import numpy as np
import ml_dtypes


def mxq(x, axis, fmt="e4m3"):
    dtype, down = {"e4m3": (ml_dtypes.float8_e4m3fn, 7), "e5m2": (ml_dtypes.float8_e5m2, 14)}[fmt]
    v = np.moveaxis(np.asarray(x, np.float32).astype(ml_dtypes.bfloat16).astype(np.float64), axis, -1)
    blocks = v.reshape(v.shape[:-1] + (-1, 32))
    amax = np.abs(blocks).max(-1, keepdims=True)
    byte = np.maximum(np.where(amax > 0, np.frexp(amax)[1] - 1 + 127, 0) - down, 1)
    scale = np.exp2(byte - 127.0)
    codes = (blocks / scale).astype(np.float32).astype(dtype).astype(np.float64)
    return np.moveaxis((codes * scale).reshape(v.shape), -1, axis)


WIDE = False


def mx_kscale(k):
    if not WIDE:
        return np.ones(k)
    levels = np.array([10, -10, 5, -5, 0])
    if k % 512:
        return np.exp2(np.random.permutation(np.resize(levels, k // 32))).repeat(32)
    a = np.empty((k // 512, 16))
    for p in range(k // 512):
        a[p, :8] = np.random.permutation(np.resize(levels, 8))
        for g in range(8):
            far = levels[np.abs(levels - a[p, g]) >= 10]
            a[p, g + 8] = far[np.random.randint(len(far))]
    return np.exp2(a.ravel()).repeat(32)


def f64(x):
    return np.asarray(x).astype(np.float64)


def striped8(idx):
    return np.concatenate([x.reshape(-1, 16).T for x in idx]).astype(np.uint16)


def runs(offs, k):
    lists = np.stack([offs[16 * r : 16 * r + 16].T.reshape(-1) for r in range(8)]).astype(np.int64)
    return lists[np.arange(k) % 512 // 64]


def pack_weight(w):
    k, n = w.shape
    w = f64(np.asarray(w, np.float32).astype(ml_dtypes.bfloat16)).reshape(k // 32, 32, n)
    amax = np.abs(w).max(1)
    byte = np.clip(np.where(amax > 0, np.frexp(amax)[1] - 1 + 127 - 7, 1), 1, 254)
    scaled = (w * np.exp2(127.0 - byte)[:, None, :]).reshape(k, n).astype(np.float32)
    words = np.ascontiguousarray(scaled.reshape(k // 512, 128, 4, n).transpose(0, 1, 3, 2)).astype(ml_dtypes.float8_e4m3fn).view(np.uint8)
    return words, np.ascontiguousarray(byte.astype(np.uint8).reshape(k // 512, 16, n))


def unpack_weight(words, scales):
    g, p, n, _ = words.shape
    vals = np.ascontiguousarray(words).view(ml_dtypes.float8_e4m3fn).astype(np.float64) * np.repeat(np.exp2(scales.astype(np.float64) - 127.0), 8, axis=1)[..., None]
    return vals.transpose(0, 1, 3, 2).reshape(g * 512, n)

def planes(y):
    n, m = y.shape
    v = y.astype(np.float32).astype(ml_dtypes.bfloat16).astype(np.float64).reshape(n // 32, 32, m)
    top = np.abs(v).max(1)
    byte = np.clip(np.where(top > 0, np.frexp(top)[1] - 1 + 127 - 7, 1), 1, 254)
    codes = (v * np.exp2(127.0 - byte)[:, None, :]).reshape(n, m).astype(np.float32).astype(ml_dtypes.float8_e4m3fn).view(np.uint8)
    words = codes.reshape(n // 512, 128, 4, m).transpose(0, 1, 3, 2)
    return np.ascontiguousarray(words), np.ascontiguousarray(byte.astype(np.uint8).reshape(n // 512, 16, m))


K, T, S, N, H = 512, 2048, 512, 512, 512


def setup_inputs():
    n = np.random.standard_normal
    s = mx_kscale(K)[:, None]
    u = mx_kscale(H)
    packed_xT = pack_weight(n((K, T)) * s)
    packed_w1 = pack_weight(n((K, H)) / np.sqrt(K) / s)
    packed_w2 = pack_weight(n((H, N)) / np.sqrt(H) / u[:, None])
    return {
        "x_words": packed_xT[0],
        "x_scales": packed_xT[1],
        "w1_words": packed_w1[0],
        "w1_scales": packed_w1[1],
        "gn": (np.random.uniform(0.5, 1.5, (H, 1)) * u[:, None]).astype(np.float32),
        "w2_words": packed_w2[0],
        "w2_scales": packed_w2[1],
        "offs": striped8(np.random.randint(0, T, (8, S))),
        "n1": striped8(np.stack([np.random.permutation(S) for _ in range(8)])),
        "n2": striped8(np.stack([np.random.permutation(S) for _ in range(8)])),
        "n3": striped8(np.stack([np.random.permutation(S) for _ in range(8)])),
        "n4": striped8(np.stack([np.random.permutation(S) for _ in range(8)])),
    }


def reference(x_words, x_scales, w1_words, w1_scales, gn, w2_words, w2_scales, offs, n1, n2, n3, n4):
    xq = unpack_weight(x_words, x_scales)[np.arange(K)[:, None], runs(offs, K)]
    y = unpack_weight(w1_words, w1_scales).T @ xq
    z = f64(gn) * ((y - (y[np.arange(H)[:, None], runs(n1, H)])) / (np.abs(y[np.arange(H)[:, None], runs(n2, H)] - y) + 0.5))
    h = unpack_weight(w2_words, w2_scales).T @ mxq(z, 0, "e4m3")
    out_0 = 0.75 * (h[np.arange(N)[:, None], runs(n3, N)] + h[np.arange(N)[:, None], runs(n4, N)]) - h
    return (out_0,) + planes(out_0)

@@ -1,0 +1,221 @@
+from contextlib import ExitStack
+
+import concourse.mybir as mybir
+
+K, T, S, N, H = 512, 2048, 512, 512, 512
+FLOPS = 2 * K * H * S + 2 * H * N * S
+
+F32 = mybir.dt.float32
+BF16 = mybir.dt.bfloat16
+I32 = mybir.dt.int32
+U32 = mybir.dt.uint32
+U16 = mybir.dt.uint16
+U8 = mybir.dt.uint8
+FP8X4 = mybir.dt.float8_e4m3fn_x4
+ALU = mybir.AluOpType
+ACT = mybir.ActivationFunctionType
+
+P = 128
+PACK = 4
+Z_CHUNKS = ((0, 256), (256, 256))
+OUT_CHUNKS = ((0, 256), (256, 128), (384, 128))
+
+
+def tile_picked_hashfraclap_none_po_kernel(
+    tc, x_words, x_scales, w1_words, w1_scales, gn, w2_words, w2_scales, offs, n1, n2, n3, n4, out_0, out_1, out_2
+):
+    nc = tc.nc
+
+    def words_of(dram):
+        return dram[0].rearrange("p c r -> p (c r)").bitcast(I32)
+
+    def entries(lst, c0, n):
+        return lst[:, c0 // 16 : (c0 + n) // 16]
+
+    def woven(bf_tile):
+        return bf_tile[:].rearrange("p (c i t) -> p c t i", i=4, t=PACK)
+
+    def unwoven(f_tile):
+        return f_tile[:].rearrange("p t (c i) -> p c t i", i=4)
+
+    with ExitStack() as ctx:
+        lists = ctx.enter_context(tc.tile_pool(name="lists", bufs=1))
+        sb = ctx.enter_context(tc.tile_pool(name="sb", bufs=1))
+        psum = ctx.enter_context(tc.psum_pool(name="psum", bufs=1))
+
+        offs_t = lists.tile([P, S // 16], U16, name="offs_t")
+        n1_t = lists.tile([P, S // 16], U16, name="n1_t")
+        n2_t = lists.tile([P, S // 16], U16, name="n2_t")
+        n3_t = lists.tile([P, S // 16], U16, name="n3_t")
+        n4_t = lists.tile([P, S // 16], U16, name="n4_t")
+
+        xw = sb.tile([P, T], U32, name="xw", align_bytes=64)
+        xs = sb.tile([P, T], U8, name="xs", align_bytes=64)
+        gw = sb.tile([P, S], U32, name="gw", align_bytes=64)
+        gs = sb.tile([P, S], U8, name="gs", align_bytes=64)
+        xplane = sb.tile([P, S], U8, name="xplane", align_bytes=64)
+        wraw = sb.tile([P, H], U32, name="wraw", align_bytes=64)
+        sraw = sb.tile([P, H], U8, name="sraw", align_bytes=64)
+        wraw2 = sb.tile([P, N], U32, name="wraw2", align_bytes=64)
+        sraw2 = sb.tile([P, N], U8, name="sraw2", align_bytes=64)
+        gain = sb.tile([P, PACK], F32, name="gain")
+        neg_gain = sb.tile([P, PACK], F32, name="neg_gain")
+        safe_gain = sb.tile([P, PACK], F32, name="safe_gain")
+        inv_gain = sb.tile([P, PACK], F32, name="inv_gain")
+        warm = sb.tile([P, 1], F32, name="warm")
+        warm_out = sb.tile([P, 1], F32, name="warm_out")
+
+        nc.vector.memset(xs[:].bitcast(I32), 0)
+        nc.vector.memset(sraw[:].bitcast(I32), 0)
+        nc.vector.memset(sraw2[:].bitcast(I32), 0)
+        nc.vector.memset(warm[:], 1.0)
+        nc.scalar.activation(warm_out[:], warm[:], ACT.Abs_reciprocal_sqrt)
+
+        nc.sync.dma_start(offs_t[:], offs)
+        nc.sync.dma_start(xs[0:P:8, :].bitcast(I32), x_scales[0].bitcast(I32))
+        nc.sync.dma_start(n2_t[:], n2)
+        for q in range(4):
+            nc.sync.dma_start(sraw[32 * q : 32 * q + 4, :].bitcast(I32), w1_scales[0, 4 * q : 4 * q + 4, :].bitcast(I32))
+        nc.sync.dma_start(xw[:].bitcast(I32), words_of(x_words))
+        nc.sync.dma_start(wraw[:].bitcast(I32), words_of(w1_words))
+        nc.sync.dma_start(n1_t[:], n1)
+        nc.sync.dma_start(n3_t[:], n3)
+        nc.sync.dma_start(n4_t[:], n4)
+        nc.gpsimd.dma_start(gain[:], gn.rearrange("(p t) o -> p (t o)", t=PACK))
+        for q in range(4):
+            nc.gpsimd.dma_start(sraw2[32 * q : 32 * q + 4, :].bitcast(I32), w2_scales[0, 4 * q : 4 * q + 4, :].bitcast(I32))
+        nc.gpsimd.dma_start(wraw2[:].bitcast(I32), words_of(w2_words))
+
+        nc.vector.tensor_copy(gs[:], xs[:].indirect(offs_t[:]))
+        nc.vector.tensor_copy(xplane[:].bitcast(I32), gs[:].bitcast(I32))
+        for r in range(1, 4):
+            nc.scalar.dma_start(xplane[r:P:32, :].bitcast(I32), gs[8 * r : P : 32, :].bitcast(I32))
+
+        nc.vector.tensor_scalar(neg_gain[:], gain[:], -1.0, None, ALU.mult)
+        nc.vector.scalar_tensor_tensor(safe_gain[:], gain[:], 0.0, gain[:], ALU.is_equal, ALU.add)
+        nc.vector.reciprocal(inv_gain[:], safe_gain[:])
+
+        def deal(name, wraw, sraw):
+            codes = sb.tile([P, H], U32, name=name + "_codes", align_bytes=64)
+            plane = sb.tile([P, H], U8, name=name + "_plane", align_bytes=64)
+            nc.vector.tensor_copy(plane[:].rearrange("p (t m) -> p t m", t=PACK), sraw[:].rearrange("p (m t) -> p t m", t=PACK))
+            nc.vector.tensor_copy(
+                codes[:].bitcast(I32).rearrange("p (t m) -> p t m", t=PACK),
+                wraw[:].bitcast(I32).rearrange("p (m t) -> p t m", t=PACK),
+            )
+            return codes, plane
+
+        nc.vector.tensor_copy(gw[:], xw[:].indirect(offs_t[:]))
+        w1c, w1p = deal("w1", wraw, sraw)
+
+        ybank = [psum.tile([P, S], F32, name="ybank%d" % t) for t in range(PACK)]
+        hbank = [psum.tile([P, S], F32, name="hbank%d" % t) for t in range(PACK)]
+        ywin = [sb.tile([P, S], F32, name="ywin%d" % t) for t in range(PACK)]
+        yown = [sb.tile([P, S], F32, name="yown%d" % t) for t in range(PACK)]
+        hwin = [sb.tile([P, S], F32, name="hwin%d" % t) for t in range(PACK)]
+        hown = [sb.tile([P, S], F32, name="hown%d" % t) for t in range(PACK)]
+        d2 = [sb.tile([P, S], F32, name="d2_%d" % t) for t in range(PACK)]
+        size = [sb.tile([P, S], F32, name="size%d" % t) for t in range(PACK)]
+        root = [sb.tile([P, S], F32, name="root%d" % t) for t in range(PACK)]
+        num = [sb.tile([P, PACK, n], F32, name="num%d" % j) for j, (c0, n) in enumerate(Z_CHUNKS)]
+        rec = [sb.tile([P, PACK, n], F32, name="rec%d" % j) for j, (c0, n) in enumerate(Z_CHUNKS)]
+        zb = [sb.tile([P, PACK * n], BF16, name="zb%d" % j, align_bytes=64) for j, (c0, n) in enumerate(Z_CHUNKS)]
+        zc = [sb.tile([P, n], U32, name="zc%d" % j, align_bytes=64) for j, (c0, n) in enumerate(Z_CHUNKS)]
+        zp = [sb.tile([P, n], U8, name="zp%d" % j, align_bytes=64) for j, (c0, n) in enumerate(Z_CHUNKS)]
+
+        for t in range(PACK):
+            cols = slice(P * t, P * (t + 1))
+            nc.tensor.matmul_mx(
+                ybank[t][:], lhsT=w1c[:, cols].bitcast(FP8X4), lhsT_scale=w1p[:, cols],
+                rhs=gw[:].bitcast(FP8X4), rhs_scale=xplane[:], start=True, stop=True,
+            )
+
+        def y_out(t):
+            nc.scalar.activation(ywin[t][:], ybank[t][:], ACT.Copy, scale=neg_gain[:, t : t + 1])
+            nc.scalar.activation(yown[t][:], ybank[t][:], ACT.Copy, scale=neg_gain[:, t : t + 1])
+
+        def gather_d2(t, j):
+            c0, n = Z_CHUNKS[j]
+            nc.vector.tensor_tensor(d2[t][:, c0 : c0 + n], ywin[t][:].indirect(entries(n2_t, c0, n)), yown[t][:, c0 : c0 + n], ALU.subtract)
+
+        def gather_num(t, j):
+            c0, n = Z_CHUNKS[j]
+            nc.vector.tensor_tensor(num[j][:, t, :], ywin[t][:].indirect(entries(n1_t, c0, n)), yown[t][:, c0 : c0 + n], ALU.subtract)
+
+        def root_of(t, c0, n):
+            nc.scalar.activation(size[t][:, c0 : c0 + n], d2[t][:, c0 : c0 + n], ACT.Abs, scale=inv_gain[:, t : t + 1])
+            nc.scalar.activation(root[t][:, c0 : c0 + n], size[t][:, c0 : c0 + n], ACT.Abs_reciprocal_sqrt, bias=0.5)
+
+        def square(t, j):
+            c0, n = Z_CHUNKS[j]
+            nc.scalar.activation(rec[j][:, t, :], root[t][:, c0 : c0 + n], ACT.Square)
+
+        def product(j):
+            nc.vector.tensor_tensor(woven(zb[j]), unwoven(num[j]), unwoven(rec[j]), ALU.mult)
+
+        def second(j):
+            c0, n = Z_CHUNKS[j]
+            nc.vector.quantize_mx(zc[j][:].bitcast(FP8X4), zp[j][:], zb[j][:])
+            for t in range(PACK):
+                cols = slice(P * t, P * (t + 1))
+                nc.tensor.matmul_mx(
+                    hbank[t][:, c0 : c0 + n], lhsT=w2c[:, cols].bitcast(FP8X4), lhsT_scale=w2p[:, cols],
+                    rhs=zc[j][:].bitcast(FP8X4), rhs_scale=zp[j][:], start=True, stop=True,
+                )
+            for t in range(PACK):
+                nc.scalar.activation(hwin[t][:, c0 : c0 + n], hbank[t][:, c0 : c0 + n], ACT.Copy, scale=0.75)
+            for t in range(PACK):
+                nc.scalar.activation(hown[t][:, c0 : c0 + n], hbank[t][:, c0 : c0 + n], ACT.Copy, scale=-1.0)
+
+        w2c, w2p = deal("w2", wraw2, sraw2)
+        for t in range(PACK):
+            y_out(t)
+        for t in range(PACK):
+            gather_d2(t, 0)
+            gather_d2(t, 1)
+            if t == 0:
+                gather_num(t, 0)
+                gather_num(t, 1)
+        for j, (c0, n) in enumerate(Z_CHUNKS):
+            for t in range(PACK):
+                root_of(t, c0, n)
+                square(t, j)
+        for t in range(1, PACK):
+            gather_num(t, 0)
+        gather_num(1, 1)
+        product(0)
+        gather_num(2, 1)
+        second(0)
+        gather_num(3, 1)
+        product(1)
+        second(1)
+
+        half = [sb.tile([P, S], F32, name="half%d" % t) for t in range(PACK)]
+        res = [sb.tile([P, PACK, n], F32, name="res%d" % j) for j, (c0, n) in enumerate(OUT_CHUNKS)]
+        ob = [sb.tile([P, PACK * n], BF16, name="ob%d" % j, align_bytes=64) for j, (c0, n) in enumerate(OUT_CHUNKS)]
+        oc = sb.tile([P, S], U32, name="oc", align_bytes=64)
+        op = sb.tile([P, S], U8, name="op", align_bytes=64)
+        out_rows = out_0.rearrange("(p t) c -> p t c", t=PACK)
+        out_words = words_of(out_1)
+
+        def finish(j):
+            c0, n = OUT_CHUNKS[j]
+            nc.vector.quantize_mx(oc[:, c0 : c0 + n].bitcast(FP8X4), op[:, c0 : c0 + n], ob[j][:])
+            nc.sync.dma_start(out_words[:, c0 : c0 + n], oc[:, c0 : c0 + n].bitcast(I32))
+
+        for j, (c0, n) in enumerate(OUT_CHUNKS):
+            for t in range(PACK):
+                nc.vector.tensor_tensor(half[t][:, c0 : c0 + n], hwin[t][:].indirect(entries(n3_t, c0, n)), hown[t][:, c0 : c0 + n], ALU.add)
+            if j > 0:
+                finish(j - 1)
+            for t in range(PACK):
+                nc.vector.tensor_tensor(res[j][:, t, :], hwin[t][:].indirect(entries(n4_t, c0, n)), half[t][:, c0 : c0 + n], ALU.add)
+            nc.sync.dma_start(out_rows[:, :, c0 : c0 + n], res[j][:])
+            if j < len(OUT_CHUNKS) - 1:
+                nc.scalar.copy(woven(ob[j]), unwoven(res[j]))
+            else:
+                nc.vector.tensor_copy(woven(ob[j]), unwoven(res[j]))
+        finish(len(OUT_CHUNKS) - 1)
+        for q in range(4):
+            queue = nc.scalar if q % 2 == 0 else nc.sync
+            queue.dma_start(out_2[0, 4 * q : 4 * q + 4, :].bitcast(I32), op[32 * q : 32 * q + 4, :].bitcast(I32))

@@ -36,7 +36,7 @@ def tile_picked_hashfraclap_none_po_kernel(
         return bf_tile[:].rearrange("p (c i t) -> p c t i", i=4, t=PACK)
 
     def unwoven(f_tile):
-        return f_tile[:].rearrange("p t (c i) -> p c t i", i=4)
+        return f_tile.rearrange("p t (c i) -> p c t i", i=4)
 
     with ExitStack() as ctx:
         lists = ctx.enter_context(tc.tile_pool(name="lists", bufs=1))
@@ -51,13 +51,11 @@ def tile_picked_hashfraclap_none_po_kernel(
 
         xw = sb.tile([P, T], U32, name="xw", align_bytes=64)
         xs = sb.tile([P, T], U8, name="xs", align_bytes=64)
-        gw = sb.tile([P, S], U32, name="gw", align_bytes=64)
-        gs = sb.tile([P, S], U8, name="gs", align_bytes=64)
-        xplane = sb.tile([P, S], U8, name="xplane", align_bytes=64)
+        gs = sb.tile([P, S], U8, name="gs", tag="picked", align_bytes=64)
+        stage = sb.tile([P, S + H], U8, name="stage", align_bytes=64)
+        planes = sb.tile([P, S + H], U8, name="planes", align_bytes=64)
         wraw = sb.tile([P, H], U32, name="wraw", align_bytes=64)
         sraw = sb.tile([P, H], U8, name="sraw", align_bytes=64)
-        wraw2 = sb.tile([P, N], U32, name="wraw2", align_bytes=64)
-        sraw2 = sb.tile([P, N], U8, name="sraw2", align_bytes=64)
         gain = sb.tile([P, PACK], F32, name="gain")
         neg_gain = sb.tile([P, PACK], F32, name="neg_gain")
         safe_gain = sb.tile([P, PACK], F32, name="safe_gain")
@@ -67,91 +65,91 @@ def tile_picked_hashfraclap_none_po_kernel(
 
         nc.vector.memset(xs[:].bitcast(I32), 0)
         nc.vector.memset(sraw[:].bitcast(I32), 0)
-        nc.vector.memset(sraw2[:].bitcast(I32), 0)
+        nc.vector.memset(planes[:].bitcast(I32), 0)
         nc.vector.memset(warm[:], 1.0)
         nc.scalar.activation(warm_out[:], warm[:], ACT.Abs_reciprocal_sqrt)
 
+        nc.scalar.dma_start(xs[0:P:8, :].bitcast(I32), x_scales[0].bitcast(I32))
+        nc.scalar.dma_start(sraw[0:P:8, :].bitcast(I32), w1_scales[0].bitcast(I32))
         nc.sync.dma_start(offs_t[:], offs)
-        nc.sync.dma_start(xs[0:P:8, :].bitcast(I32), x_scales[0].bitcast(I32))
         nc.sync.dma_start(n2_t[:], n2)
-        for q in range(4):
-            nc.sync.dma_start(sraw[32 * q : 32 * q + 4, :].bitcast(I32), w1_scales[0, 4 * q : 4 * q + 4, :].bitcast(I32))
-        nc.sync.dma_start(xw[:].bitcast(I32), words_of(x_words))
-        nc.sync.dma_start(wraw[:].bitcast(I32), words_of(w1_words))
         nc.sync.dma_start(n1_t[:], n1)
         nc.sync.dma_start(n3_t[:], n3)
         nc.sync.dma_start(n4_t[:], n4)
+        nc.sync.dma_start(xw[:].bitcast(I32), words_of(x_words))
+        nc.sync.dma_start(wraw[:].bitcast(I32), words_of(w1_words))
         nc.gpsimd.dma_start(gain[:], gn.rearrange("(p t) o -> p (t o)", t=PACK))
-        for q in range(4):
-            nc.gpsimd.dma_start(sraw2[32 * q : 32 * q + 4, :].bitcast(I32), w2_scales[0, 4 * q : 4 * q + 4, :].bitcast(I32))
-        nc.gpsimd.dma_start(wraw2[:].bitcast(I32), words_of(w2_words))
+
+        def deal_bytes(dst):
+            nc.vector.tensor_copy(dst.rearrange("p (t m) -> p t m", t=PACK), sraw[:].rearrange("p (m t) -> p t m", t=PACK))
+
+        def deal_words(dst):
+            nc.vector.tensor_copy(
+                dst.bitcast(I32).rearrange("p (t m) -> p t m", t=PACK),
+                wraw[:].bitcast(I32).rearrange("p (m t) -> p t m", t=PACK),
+            )
 
         nc.vector.tensor_copy(gs[:], xs[:].indirect(offs_t[:]))
-        nc.vector.tensor_copy(xplane[:].bitcast(I32), gs[:].bitcast(I32))
-        for r in range(1, 4):
-            nc.scalar.dma_start(xplane[r:P:32, :].bitcast(I32), gs[8 * r : P : 32, :].bitcast(I32))
+        deal_bytes(stage[:, S:])
+        nc.vector.tensor_copy(stage[:, :S].bitcast(I32), gs[:].bitcast(I32))
+        for q in range(4):
+            nc.scalar.dma_start(planes[32 * q : 32 * q + 4, :].bitcast(I32), stage[32 * q : 32 * q + 32 : 8, :].bitcast(I32))
 
         nc.vector.tensor_scalar(neg_gain[:], gain[:], -1.0, None, ALU.mult)
         nc.vector.scalar_tensor_tensor(safe_gain[:], gain[:], 0.0, gain[:], ALU.is_equal, ALU.add)
         nc.vector.reciprocal(inv_gain[:], safe_gain[:])
 
-        def deal(name, wraw, sraw):
-            codes = sb.tile([P, H], U32, name=name + "_codes", align_bytes=64)
-            plane = sb.tile([P, H], U8, name=name + "_plane", align_bytes=64)
-            nc.vector.tensor_copy(plane[:].rearrange("p (t m) -> p t m", t=PACK), sraw[:].rearrange("p (m t) -> p t m", t=PACK))
-            nc.vector.tensor_copy(
-                codes[:].bitcast(I32).rearrange("p (t m) -> p t m", t=PACK),
-                wraw[:].bitcast(I32).rearrange("p (m t) -> p t m", t=PACK),
-            )
-            return codes, plane
-
+        w1c = sb.tile([P, H], U32, name="w1c", align_bytes=64)
+        w2c = sb.tile([P, N], U32, name="w2c", align_bytes=64)
+        w2p = sb.tile([P, N], U8, name="w2p", align_bytes=64)
+        gw = sb.tile([P, S], U32, name="gw", tag="picked", align_bytes=64)
         nc.vector.tensor_copy(gw[:], xw[:].indirect(offs_t[:]))
-        w1c, w1p = deal("w1", wraw, sraw)
+        deal_words(w1c[:])
+        nc.sync.dma_start(wraw[:].bitcast(I32), words_of(w2_words))
+        for q in range(4):
+            nc.sync.dma_start(sraw[32 * q : 32 * q + 4, :].bitcast(I32), w2_scales[0, 4 * q : 4 * q + 4, :].bitcast(I32))
 
         ybank = [psum.tile([P, S], F32, name="ybank%d" % t) for t in range(PACK)]
-        hbank = [psum.tile([P, S], F32, name="hbank%d" % t) for t in range(PACK)]
-        ywin = [sb.tile([P, S], F32, name="ywin%d" % t) for t in range(PACK)]
-        yown = [sb.tile([P, S], F32, name="yown%d" % t) for t in range(PACK)]
+        hbank = [[psum.tile([P, 2, n], F32, name="hbank%d_%d" % (j, u)) for u in range(2)] for j, (c0, n) in enumerate(Z_CHUNKS)]
+        ywin = [sb.tile([P, 2 * S], F32, name="ywin%d" % t) for t in range(PACK)]
+        ylast = sb.tile([P, S], F32, name="ylast")
+        yown = [ywin[t + 1][:, S:] for t in range(PACK - 1)] + [ylast[:]]
+        nc.vector.memset(ywin[0][:, S:], 0.0)
         hwin = [sb.tile([P, S], F32, name="hwin%d" % t) for t in range(PACK)]
-        hown = [sb.tile([P, S], F32, name="hown%d" % t) for t in range(PACK)]
         d2 = [sb.tile([P, S], F32, name="d2_%d" % t) for t in range(PACK)]
         size = [sb.tile([P, S], F32, name="size%d" % t) for t in range(PACK)]
         root = [sb.tile([P, S], F32, name="root%d" % t) for t in range(PACK)]
-        num = [sb.tile([P, PACK, n], F32, name="num%d" % j) for j, (c0, n) in enumerate(Z_CHUNKS)]
-        rec = [sb.tile([P, PACK, n], F32, name="rec%d" % j) for j, (c0, n) in enumerate(Z_CHUNKS)]
-        zb = [sb.tile([P, PACK * n], BF16, name="zb%d" % j, align_bytes=64) for j, (c0, n) in enumerate(Z_CHUNKS)]
+        num = sb.tile([P, PACK, S], F32, name="num")
+        rec = sb.tile([P, PACK, S], F32, name="rec")
         zc = [sb.tile([P, n], U32, name="zc%d" % j, align_bytes=64) for j, (c0, n) in enumerate(Z_CHUNKS)]
         zp = [sb.tile([P, n], U8, name="zp%d" % j, align_bytes=64) for j, (c0, n) in enumerate(Z_CHUNKS)]
+        zb = [sb.tile([P, PACK * n], BF16, name="zb%d" % j, tag="zb%d" % j, align_bytes=64) for j, (c0, n) in enumerate(Z_CHUNKS)]
 
         for t in range(PACK):
             cols = slice(P * t, P * (t + 1))
             nc.tensor.matmul_mx(
-                ybank[t][:], lhsT=w1c[:, cols].bitcast(FP8X4), lhsT_scale=w1p[:, cols],
-                rhs=gw[:].bitcast(FP8X4), rhs_scale=xplane[:], start=True, stop=True,
+                ybank[t][:], lhsT=w1c[:, cols].bitcast(FP8X4), lhsT_scale=planes[:, S + P * t : S + P * (t + 1)],
+                rhs=gw[:].bitcast(FP8X4), rhs_scale=planes[:, :S], start=True, stop=True,
             )
 
         def y_out(t):
-            nc.scalar.activation(ywin[t][:], ybank[t][:], ACT.Copy, scale=neg_gain[:, t : t + 1])
-            nc.scalar.activation(yown[t][:], ybank[t][:], ACT.Copy, scale=neg_gain[:, t : t + 1])
+            nc.scalar.activation(ywin[t][:, :S], ybank[t][:], ACT.Copy, scale=neg_gain[:, t : t + 1])
+            nc.scalar.activation(yown[t], ybank[t][:], ACT.Copy, scale=neg_gain[:, t : t + 1])
 
-        def gather_d2(t, j):
-            c0, n = Z_CHUNKS[j]
+        def gather_d2(t, c0, n):
             nc.vector.tensor_tensor(d2[t][:, c0 : c0 + n], ywin[t][:].indirect(entries(n2_t, c0, n)), yown[t][:, c0 : c0 + n], ALU.subtract)
 
-        def gather_num(t, j):
-            c0, n = Z_CHUNKS[j]
-            nc.vector.tensor_tensor(num[j][:, t, :], ywin[t][:].indirect(entries(n1_t, c0, n)), yown[t][:, c0 : c0 + n], ALU.subtract)
+        def gather_num(t, c0, n):
+            nc.vector.tensor_tensor(num[:, t, c0 : c0 + n], ywin[t][:].indirect(entries(n1_t, c0, n)), yown[t][:, c0 : c0 + n], ALU.subtract)
 
-        def root_of(t, c0, n):
+        def inverse(t, c0, n):
             nc.scalar.activation(size[t][:, c0 : c0 + n], d2[t][:, c0 : c0 + n], ACT.Abs, scale=inv_gain[:, t : t + 1])
             nc.scalar.activation(root[t][:, c0 : c0 + n], size[t][:, c0 : c0 + n], ACT.Abs_reciprocal_sqrt, bias=0.5)
-
-        def square(t, j):
-            c0, n = Z_CHUNKS[j]
-            nc.scalar.activation(rec[j][:, t, :], root[t][:, c0 : c0 + n], ACT.Square)
+            nc.scalar.activation(rec[:, t, c0 : c0 + n], root[t][:, c0 : c0 + n], ACT.Square)
 
         def product(j):
-            nc.vector.tensor_tensor(woven(zb[j]), unwoven(num[j]), unwoven(rec[j]), ALU.mult)
+            c0, n = Z_CHUNKS[j]
+            nc.vector.tensor_tensor(woven(zb[j]), unwoven(num[:, :, c0 : c0 + n]), unwoven(rec[:, :, c0 : c0 + n]), ALU.mult)
 
         def second(j):
             c0, n = Z_CHUNKS[j]
@@ -159,36 +157,39 @@ def tile_picked_hashfraclap_none_po_kernel(
             for t in range(PACK):
                 cols = slice(P * t, P * (t + 1))
                 nc.tensor.matmul_mx(
-                    hbank[t][:, c0 : c0 + n], lhsT=w2c[:, cols].bitcast(FP8X4), lhsT_scale=w2p[:, cols],
+                    hbank[j][t // 2][:, t % 2, :], lhsT=w2c[:, cols].bitcast(FP8X4), lhsT_scale=w2p[:, cols],
                     rhs=zc[j][:].bitcast(FP8X4), rhs_scale=zp[j][:], start=True, stop=True,
                 )
             for t in range(PACK):
-                nc.scalar.activation(hwin[t][:, c0 : c0 + n], hbank[t][:, c0 : c0 + n], ACT.Copy, scale=0.75)
-            for t in range(PACK):
-                nc.scalar.activation(hown[t][:, c0 : c0 + n], hbank[t][:, c0 : c0 + n], ACT.Copy, scale=-1.0)
+                nc.scalar.activation(hwin[t][:, c0 : c0 + n], hbank[j][t // 2][:, t % 2, :], ACT.Copy, scale=0.75)
 
-        w2c, w2p = deal("w2", wraw2, sraw2)
-        for t in range(PACK):
-            y_out(t)
-        for t in range(PACK):
-            gather_d2(t, 0)
-            gather_d2(t, 1)
-            if t == 0:
-                gather_num(t, 0)
-                gather_num(t, 1)
-        for j, (c0, n) in enumerate(Z_CHUNKS):
-            for t in range(PACK):
-                root_of(t, c0, n)
-                square(t, j)
-        for t in range(1, PACK):
-            gather_num(t, 0)
-        gather_num(1, 1)
+        y_out(0)
+        deal_bytes(w2p[:])
+        deal_words(w2c[:])
+        for t in range(PACK - 1):
+            y_out(t + 1)
+            gather_d2(t, 0, S)
+            inverse(t, 0, S)
+            gather_num(t, 0, S)
+        last = PACK - 1
+        for c0, n in Z_CHUNKS:
+            gather_d2(last, c0, n)
+            inverse(last, c0, n)
+        gather_num(last, *Z_CHUNKS[0])
         product(0)
-        gather_num(2, 1)
+        gather_num(last, *Z_CHUNKS[1])
         second(0)
-        gather_num(3, 1)
         product(1)
         second(1)
+        hown = [sb.tile([P, PACK, n], F32, name="hown%d" % j, tag="zb%d" % (1 - j), align_bytes=64) for j, (c0, n) in enumerate(Z_CHUNKS)]
+        for u in range(2):
+            nc.vector.tensor_scalar(hown[0][:, 2 * u : 2 * u + 2, :], hbank[0][u][:], -1.0, None, ALU.mult)
+        for u in range(2):
+            nc.scalar.activation(hown[1][:, 2 * u : 2 * u + 2, :], hbank[1][u][:], ACT.Copy, scale=-1.0)
+
+        def own(t, c0, n):
+            j = c0 // 256
+            return hown[j][:, t, c0 - 256 * j : c0 - 256 * j + n]
 
         half = [sb.tile([P, S], F32, name="half%d" % t) for t in range(PACK)]
         res = [sb.tile([P, PACK, n], F32, name="res%d" % j) for j, (c0, n) in enumerate(OUT_CHUNKS)]
@@ -205,16 +206,16 @@ def tile_picked_hashfraclap_none_po_kernel(
 
         for j, (c0, n) in enumerate(OUT_CHUNKS):
             for t in range(PACK):
-                nc.vector.tensor_tensor(half[t][:, c0 : c0 + n], hwin[t][:].indirect(entries(n3_t, c0, n)), hown[t][:, c0 : c0 + n], ALU.add)
+                nc.vector.tensor_tensor(half[t][:, c0 : c0 + n], hwin[t][:].indirect(entries(n3_t, c0, n)), own(t, c0, n), ALU.add)
             if j > 0:
                 finish(j - 1)
             for t in range(PACK):
                 nc.vector.tensor_tensor(res[j][:, t, :], hwin[t][:].indirect(entries(n4_t, c0, n)), half[t][:, c0 : c0 + n], ALU.add)
             nc.sync.dma_start(out_rows[:, :, c0 : c0 + n], res[j][:])
             if j < len(OUT_CHUNKS) - 1:
-                nc.scalar.copy(woven(ob[j]), unwoven(res[j]))
+                nc.scalar.copy(woven(ob[j]), unwoven(res[j][:]))
             else:
-                nc.vector.tensor_copy(woven(ob[j]), unwoven(res[j]))
+                nc.vector.tensor_copy(woven(ob[j]), unwoven(res[j][:]))
         finish(len(OUT_CHUNKS) - 1)
         for q in range(4):
             queue = nc.scalar if q % 2 == 0 else nc.sync

@@ -63,22 +63,23 @@ def tile_picked_hashfraclap_none_po_kernel(
         warm = sb.tile([P, 1], F32, name="warm")
         warm_out = sb.tile([P, 1], F32, name="warm_out")
 
-        nc.vector.memset(xs[:].bitcast(I32), 0)
+        nc.gpsimd.memset(xs[:, : T // 2].bitcast(I32), 0)
+        nc.vector.memset(xs[:, T // 2 :].bitcast(I32), 0)
         nc.vector.memset(sraw[:].bitcast(I32), 0)
-        nc.vector.memset(planes[:].bitcast(I32), 0)
         nc.vector.memset(warm[:], 1.0)
+        nc.vector.memset(planes[:].bitcast(I32), 0)
         nc.scalar.activation(warm_out[:], warm[:], ACT.Abs_reciprocal_sqrt)
 
-        nc.scalar.dma_start(xs[0:P:8, :].bitcast(I32), x_scales[0].bitcast(I32))
-        nc.scalar.dma_start(sraw[0:P:8, :].bitcast(I32), w1_scales[0].bitcast(I32))
         nc.sync.dma_start(offs_t[:], offs)
+        nc.sync.dma_start(xs[0:P:8, :].bitcast(I32), x_scales[0].bitcast(I32))
+        nc.sync.dma_start(sraw[0:P:8, :].bitcast(I32), w1_scales[0].bitcast(I32))
         nc.sync.dma_start(n2_t[:], n2)
         nc.sync.dma_start(n1_t[:], n1)
+        nc.sync.dma_start(gain[:], gn.rearrange("(p t) o -> p (t o)", t=PACK))
+        nc.sync.dma_start(wraw[:].bitcast(I32), words_of(w1_words))
+        nc.sync.dma_start(xw[:].bitcast(I32), words_of(x_words))
         nc.sync.dma_start(n3_t[:], n3)
         nc.sync.dma_start(n4_t[:], n4)
-        nc.sync.dma_start(xw[:].bitcast(I32), words_of(x_words))
-        nc.sync.dma_start(wraw[:].bitcast(I32), words_of(w1_words))
-        nc.gpsimd.dma_start(gain[:], gn.rearrange("(p t) o -> p (t o)", t=PACK))
 
         def deal_bytes(dst):
             nc.vector.tensor_copy(dst.rearrange("p (t m) -> p t m", t=PACK), sraw[:].rearrange("p (m t) -> p t m", t=PACK))
@@ -109,8 +110,10 @@ def tile_picked_hashfraclap_none_po_kernel(
         for q in range(4):
             nc.sync.dma_start(sraw[32 * q : 32 * q + 4, :].bitcast(I32), w2_scales[0, 4 * q : 4 * q + 4, :].bitcast(I32))
 
-        ybank = [psum.tile([P, S], F32, name="ybank%d" % t) for t in range(PACK)]
-        hbank = [[psum.tile([P, 2, n], F32, name="hbank%d_%d" % (j, u)) for u in range(2)] for j, (c0, n) in enumerate(Z_CHUNKS)]
+        half_s = S // 2
+        first = [psum.tile([P, half_s], F32, name="first%d" % u, tag="bank%d" % (4 * u)) for u in range(2)]
+        ybank = [None] + [psum.tile([P, S], F32, name="ybank%d" % t, tag="bank%d" % t) for t in range(1, PACK)]
+        hearly = [psum.tile([P, 2, half_s], F32, name="hearly%d" % u, tag="bank%d" % (5 + u)) for u in range(2)]
         ywin = [sb.tile([P, 2 * S], F32, name="ywin%d" % t) for t in range(PACK)]
         ylast = sb.tile([P, S], F32, name="ylast")
         yown = [ywin[t + 1][:, S:] for t in range(PACK - 1)] + [ylast[:]]
@@ -125,12 +128,21 @@ def tile_picked_hashfraclap_none_po_kernel(
         zp = [sb.tile([P, n], U8, name="zp%d" % j, align_bytes=64) for j, (c0, n) in enumerate(Z_CHUNKS)]
         zb = [sb.tile([P, PACK * n], BF16, name="zb%d" % j, tag="zb%d" % j, align_bytes=64) for j, (c0, n) in enumerate(Z_CHUNKS)]
 
-        for t in range(PACK):
-            cols = slice(P * t, P * (t + 1))
+        def first_product(bank, t, c0, n):
             nc.tensor.matmul_mx(
-                ybank[t][:], lhsT=w1c[:, cols].bitcast(FP8X4), lhsT_scale=planes[:, S + P * t : S + P * (t + 1)],
-                rhs=gw[:].bitcast(FP8X4), rhs_scale=planes[:, :S], start=True, stop=True,
+                bank, lhsT=w1c[:, P * t : P * (t + 1)].bitcast(FP8X4), lhsT_scale=planes[:, S + P * t : S + P * (t + 1)],
+                rhs=gw[:, c0 : c0 + n].bitcast(FP8X4), rhs_scale=planes[:, c0 : c0 + n], start=True, stop=True,
             )
+
+        for u in range(2):
+            first_product(first[u][:], 0, u * half_s, half_s)
+        for t in range(1, PACK):
+            first_product(ybank[t][:], t, 0, S)
+
+        nc.scalar.activation(ywin[0][:, :half_s], first[0][:], ACT.Copy, scale=neg_gain[:, 0:1])
+        nc.vector.tensor_scalar(ywin[0][:, half_s:S], first[1][:], neg_gain[:, 0:1], None, ALU.mult)
+        nc.scalar.activation(yown[0][:, :half_s], first[0][:], ACT.Copy, scale=neg_gain[:, 0:1])
+        nc.vector.tensor_scalar(yown[0][:, half_s:], first[1][:], neg_gain[:, 0:1], None, ALU.mult)
 
         def y_out(t):
             nc.scalar.activation(ywin[t][:, :S], ybank[t][:], ACT.Copy, scale=neg_gain[:, t : t + 1])
@@ -151,19 +163,18 @@ def tile_picked_hashfraclap_none_po_kernel(
             c0, n = Z_CHUNKS[j]
             nc.vector.tensor_tensor(woven(zb[j]), unwoven(num[:, :, c0 : c0 + n]), unwoven(rec[:, :, c0 : c0 + n]), ALU.mult)
 
-        def second(j):
+        def second(j, banks):
             c0, n = Z_CHUNKS[j]
             nc.vector.quantize_mx(zc[j][:].bitcast(FP8X4), zp[j][:], zb[j][:])
             for t in range(PACK):
                 cols = slice(P * t, P * (t + 1))
                 nc.tensor.matmul_mx(
-                    hbank[j][t // 2][:, t % 2, :], lhsT=w2c[:, cols].bitcast(FP8X4), lhsT_scale=w2p[:, cols],
+                    banks[t], lhsT=w2c[:, cols].bitcast(FP8X4), lhsT_scale=w2p[:, cols],
                     rhs=zc[j][:].bitcast(FP8X4), rhs_scale=zp[j][:], start=True, stop=True,
                 )
             for t in range(PACK):
-                nc.scalar.activation(hwin[t][:, c0 : c0 + n], hbank[j][t // 2][:, t % 2, :], ACT.Copy, scale=0.75)
+                nc.scalar.activation(hwin[t][:, c0 : c0 + n], banks[t], ACT.Copy, scale=0.75)
 
-        y_out(0)
         deal_bytes(w2p[:])
         deal_words(w2c[:])
         for t in range(PACK - 1):
@@ -178,14 +189,15 @@ def tile_picked_hashfraclap_none_po_kernel(
         gather_num(last, *Z_CHUNKS[0])
         product(0)
         gather_num(last, *Z_CHUNKS[1])
-        second(0)
+        second(0, [hearly[t // 2][:, t % 2, :] for t in range(PACK)])
         product(1)
-        second(1)
+        hlate = [psum.tile([P, half_s], F32, name="hlate%d" % t, tag="bank%d" % t) for t in range(PACK)]
+        second(1, [bank[:] for bank in hlate])
         hown = [sb.tile([P, PACK, n], F32, name="hown%d" % j, tag="zb%d" % (1 - j), align_bytes=64) for j, (c0, n) in enumerate(Z_CHUNKS)]
         for u in range(2):
-            nc.vector.tensor_scalar(hown[0][:, 2 * u : 2 * u + 2, :], hbank[0][u][:], -1.0, None, ALU.mult)
-        for u in range(2):
-            nc.scalar.activation(hown[1][:, 2 * u : 2 * u + 2, :], hbank[1][u][:], ACT.Copy, scale=-1.0)
+            nc.vector.tensor_scalar(hown[0][:, 2 * u : 2 * u + 2, :], hearly[u][:], -1.0, None, ALU.mult)
+        for t in range(PACK):
+            nc.scalar.activation(hown[1][:, t, :], hlate[t][:], ACT.Copy, scale=-1.0)
 
         def own(t, c0, n):
             j = c0 // 256

from contextlib import ExitStack

import concourse.mybir as mybir

K, T, S, N, H = 512, 2048, 512, 512, 512
FLOPS = 2 * K * H * S + 2 * H * N * S

F32 = mybir.dt.float32
BF16 = mybir.dt.bfloat16
I32 = mybir.dt.int32
U32 = mybir.dt.uint32
U16 = mybir.dt.uint16
U8 = mybir.dt.uint8
FP8X4 = mybir.dt.float8_e4m3fn_x4
ALU = mybir.AluOpType
ACT = mybir.ActivationFunctionType

P = 128
PACK = 4
Z_CHUNKS = ((0, 256), (256, 256))
OUT_CHUNKS = ((0, 256), (256, 128), (384, 128))


def tile_picked_hashfraclap_none_po_kernel(
    tc, x_words, x_scales, w1_words, w1_scales, gn, w2_words, w2_scales, offs, n1, n2, n3, n4, out_0, out_1, out_2
):
    nc = tc.nc

    def words_of(dram):
        return dram[0].rearrange("p c r -> p (c r)").bitcast(I32)

    def entries(lst, c0, n):
        return lst[:, c0 // 16 : (c0 + n) // 16]

    def woven(bf_tile):
        return bf_tile[:].rearrange("p (c i t) -> p c t i", i=4, t=PACK)

    def unwoven(f_tile):
        return f_tile.rearrange("p t (c i) -> p c t i", i=4)

    with ExitStack() as ctx:
        lists = ctx.enter_context(tc.tile_pool(name="lists", bufs=1))
        sb = ctx.enter_context(tc.tile_pool(name="sb", bufs=1))
        psum = ctx.enter_context(tc.psum_pool(name="psum", bufs=1))

        offs_t = lists.tile([P, S // 16], U16, name="offs_t")
        n1_t = lists.tile([P, S // 16], U16, name="n1_t")
        n2_t = lists.tile([P, S // 16], U16, name="n2_t")
        n3_t = lists.tile([P, S // 16], U16, name="n3_t")
        n4_t = lists.tile([P, S // 16], U16, name="n4_t")

        xw = sb.tile([P, T], U32, name="xw", align_bytes=64)
        xs = sb.tile([P, T], U8, name="xs", align_bytes=64)
        gs = sb.tile([P, S], U8, name="gs", tag="picked", align_bytes=64)
        stage = sb.tile([P, S + H], U8, name="stage", align_bytes=64)
        planes = sb.tile([P, S + H], U8, name="planes", align_bytes=64)
        wraw = sb.tile([P, H], U32, name="wraw", align_bytes=64)
        sraw = sb.tile([P, H], U8, name="sraw", align_bytes=64)
        gain = sb.tile([P, PACK], F32, name="gain")
        neg_gain = sb.tile([P, PACK], F32, name="neg_gain")
        safe_gain = sb.tile([P, PACK], F32, name="safe_gain")
        inv_gain = sb.tile([P, PACK], F32, name="inv_gain")
        warm = sb.tile([P, 1], F32, name="warm")
        warm_out = sb.tile([P, 1], F32, name="warm_out")

        nc.gpsimd.memset(xs[:, : T // 2].bitcast(I32), 0)
        nc.vector.memset(xs[:, T // 2 :].bitcast(I32), 0)
        nc.vector.memset(sraw[:].bitcast(I32), 0)
        nc.vector.memset(warm[:], 1.0)
        nc.vector.memset(planes[:].bitcast(I32), 0)
        nc.scalar.activation(warm_out[:], warm[:], ACT.Abs_reciprocal_sqrt)

        nc.sync.dma_start(offs_t[:], offs)
        nc.sync.dma_start(xs[0:P:8, :].bitcast(I32), x_scales[0].bitcast(I32))
        nc.sync.dma_start(sraw[0:P:8, :].bitcast(I32), w1_scales[0].bitcast(I32))
        nc.sync.dma_start(n2_t[:], n2)
        nc.sync.dma_start(n1_t[:], n1)
        nc.sync.dma_start(gain[:], gn.rearrange("(p t) o -> p (t o)", t=PACK))
        nc.sync.dma_start(wraw[:].bitcast(I32), words_of(w1_words))
        nc.sync.dma_start(xw[:].bitcast(I32), words_of(x_words))
        nc.sync.dma_start(n3_t[:], n3)
        nc.sync.dma_start(n4_t[:], n4)

        def deal_bytes(dst):
            nc.vector.tensor_copy(dst.rearrange("p (t m) -> p t m", t=PACK), sraw[:].rearrange("p (m t) -> p t m", t=PACK))

        def deal_words(dst):
            nc.vector.tensor_copy(
                dst.bitcast(I32).rearrange("p (t m) -> p t m", t=PACK),
                wraw[:].bitcast(I32).rearrange("p (m t) -> p t m", t=PACK),
            )

        nc.vector.tensor_copy(gs[:], xs[:].indirect(offs_t[:]))
        deal_bytes(stage[:, S:])
        nc.vector.tensor_copy(stage[:, :S].bitcast(I32), gs[:].bitcast(I32))
        for q in range(4):
            nc.scalar.dma_start(planes[32 * q : 32 * q + 4, :].bitcast(I32), stage[32 * q : 32 * q + 32 : 8, :].bitcast(I32))

        nc.vector.tensor_scalar(neg_gain[:], gain[:], -1.0, None, ALU.mult)
        nc.vector.scalar_tensor_tensor(safe_gain[:], gain[:], 0.0, gain[:], ALU.is_equal, ALU.add)
        nc.vector.reciprocal(inv_gain[:], safe_gain[:])

        w1c = sb.tile([P, H], U32, name="w1c", align_bytes=64)
        w2c = sb.tile([P, N], U32, name="w2c", align_bytes=64)
        w2p = sb.tile([P, N], U8, name="w2p", align_bytes=64)
        gw = sb.tile([P, S], U32, name="gw", tag="picked", align_bytes=64)
        nc.vector.tensor_copy(gw[:], xw[:].indirect(offs_t[:]))
        deal_words(w1c[:])
        nc.sync.dma_start(wraw[:].bitcast(I32), words_of(w2_words))
        for q in range(4):
            nc.sync.dma_start(sraw[32 * q : 32 * q + 4, :].bitcast(I32), w2_scales[0, 4 * q : 4 * q + 4, :].bitcast(I32))

        half_s = S // 2
        first = [psum.tile([P, half_s], F32, name="first%d" % u, tag="bank%d" % (4 * u)) for u in range(2)]
        ybank = [None] + [psum.tile([P, S], F32, name="ybank%d" % t, tag="bank%d" % t) for t in range(1, PACK)]
        hearly = [psum.tile([P, 2, half_s], F32, name="hearly%d" % u, tag="bank%d" % (5 + u)) for u in range(2)]
        ywin = [sb.tile([P, 2 * S], F32, name="ywin%d" % t) for t in range(PACK)]
        ylast = sb.tile([P, S], F32, name="ylast")
        yown = [ywin[t + 1][:, S:] for t in range(PACK - 1)] + [ylast[:]]
        nc.vector.memset(ywin[0][:, S:], 0.0)
        hwin = [sb.tile([P, S], F32, name="hwin%d" % t) for t in range(PACK)]
        d2 = [sb.tile([P, S], F32, name="d2_%d" % t) for t in range(PACK)]
        size = [sb.tile([P, S], F32, name="size%d" % t) for t in range(PACK)]
        root = [sb.tile([P, S], F32, name="root%d" % t) for t in range(PACK)]
        num = sb.tile([P, PACK, S], F32, name="num")
        rec = sb.tile([P, PACK, S], F32, name="rec")
        zc = [sb.tile([P, n], U32, name="zc%d" % j, align_bytes=64) for j, (c0, n) in enumerate(Z_CHUNKS)]
        zp = [sb.tile([P, n], U8, name="zp%d" % j, align_bytes=64) for j, (c0, n) in enumerate(Z_CHUNKS)]
        zb = [sb.tile([P, PACK * n], BF16, name="zb%d" % j, tag="zb%d" % j, align_bytes=64) for j, (c0, n) in enumerate(Z_CHUNKS)]

        def first_product(bank, t, c0, n):
            nc.tensor.matmul_mx(
                bank, lhsT=w1c[:, P * t : P * (t + 1)].bitcast(FP8X4), lhsT_scale=planes[:, S + P * t : S + P * (t + 1)],
                rhs=gw[:, c0 : c0 + n].bitcast(FP8X4), rhs_scale=planes[:, c0 : c0 + n], start=True, stop=True,
            )

        for u in range(2):
            first_product(first[u][:], 0, u * half_s, half_s)
        for t in range(1, PACK):
            first_product(ybank[t][:], t, 0, S)

        nc.scalar.activation(ywin[0][:, :half_s], first[0][:], ACT.Copy, scale=neg_gain[:, 0:1])
        nc.vector.tensor_scalar(ywin[0][:, half_s:S], first[1][:], neg_gain[:, 0:1], None, ALU.mult)
        nc.scalar.activation(yown[0][:, :half_s], first[0][:], ACT.Copy, scale=neg_gain[:, 0:1])
        nc.vector.tensor_scalar(yown[0][:, half_s:], first[1][:], neg_gain[:, 0:1], None, ALU.mult)

        def y_out(t):
            nc.scalar.activation(ywin[t][:, :S], ybank[t][:], ACT.Copy, scale=neg_gain[:, t : t + 1])
            nc.scalar.activation(yown[t], ybank[t][:], ACT.Copy, scale=neg_gain[:, t : t + 1])

        def gather_d2(t, c0, n):
            nc.vector.tensor_tensor(d2[t][:, c0 : c0 + n], ywin[t][:].indirect(entries(n2_t, c0, n)), yown[t][:, c0 : c0 + n], ALU.subtract)

        def gather_num(t, c0, n):
            nc.vector.tensor_tensor(num[:, t, c0 : c0 + n], ywin[t][:].indirect(entries(n1_t, c0, n)), yown[t][:, c0 : c0 + n], ALU.subtract)

        def inverse(t, c0, n):
            nc.scalar.activation(size[t][:, c0 : c0 + n], d2[t][:, c0 : c0 + n], ACT.Abs, scale=inv_gain[:, t : t + 1])
            nc.scalar.activation(root[t][:, c0 : c0 + n], size[t][:, c0 : c0 + n], ACT.Abs_reciprocal_sqrt, bias=0.5)
            nc.scalar.activation(rec[:, t, c0 : c0 + n], root[t][:, c0 : c0 + n], ACT.Square)

        def product(j):
            c0, n = Z_CHUNKS[j]
            nc.vector.tensor_tensor(woven(zb[j]), unwoven(num[:, :, c0 : c0 + n]), unwoven(rec[:, :, c0 : c0 + n]), ALU.mult)

        def second(j, banks):
            c0, n = Z_CHUNKS[j]
            nc.vector.quantize_mx(zc[j][:].bitcast(FP8X4), zp[j][:], zb[j][:])
            for t in range(PACK):
                cols = slice(P * t, P * (t + 1))
                nc.tensor.matmul_mx(
                    banks[t], lhsT=w2c[:, cols].bitcast(FP8X4), lhsT_scale=w2p[:, cols],
                    rhs=zc[j][:].bitcast(FP8X4), rhs_scale=zp[j][:], start=True, stop=True,
                )
            for t in range(PACK):
                nc.scalar.activation(hwin[t][:, c0 : c0 + n], banks[t], ACT.Copy, scale=0.75)

        deal_bytes(w2p[:])
        deal_words(w2c[:])
        for t in range(PACK - 1):
            y_out(t + 1)
            gather_d2(t, 0, S)
            inverse(t, 0, S)
            gather_num(t, 0, S)
        last = PACK - 1
        for c0, n in Z_CHUNKS:
            gather_d2(last, c0, n)
            inverse(last, c0, n)
        gather_num(last, *Z_CHUNKS[0])
        product(0)
        gather_num(last, *Z_CHUNKS[1])
        second(0, [hearly[t // 2][:, t % 2, :] for t in range(PACK)])
        product(1)
        hlate = [psum.tile([P, half_s], F32, name="hlate%d" % t, tag="bank%d" % t) for t in range(PACK)]
        second(1, [bank[:] for bank in hlate])
        hown = [sb.tile([P, PACK, n], F32, name="hown%d" % j, tag="zb%d" % (1 - j), align_bytes=64) for j, (c0, n) in enumerate(Z_CHUNKS)]
        for u in range(2):
            nc.vector.tensor_scalar(hown[0][:, 2 * u : 2 * u + 2, :], hearly[u][:], -1.0, None, ALU.mult)
        for t in range(PACK):
            nc.scalar.activation(hown[1][:, t, :], hlate[t][:], ACT.Copy, scale=-1.0)

        def own(t, c0, n):
            j = c0 // 256
            return hown[j][:, t, c0 - 256 * j : c0 - 256 * j + n]

        half = [sb.tile([P, S], F32, name="half%d" % t) for t in range(PACK)]
        res = [sb.tile([P, PACK, n], F32, name="res%d" % j) for j, (c0, n) in enumerate(OUT_CHUNKS)]
        ob = [sb.tile([P, PACK * n], BF16, name="ob%d" % j, align_bytes=64) for j, (c0, n) in enumerate(OUT_CHUNKS)]
        oc = sb.tile([P, S], U32, name="oc", align_bytes=64)
        op = sb.tile([P, S], U8, name="op", align_bytes=64)
        out_rows = out_0.rearrange("(p t) c -> p t c", t=PACK)
        out_words = words_of(out_1)

        def finish(j):
            c0, n = OUT_CHUNKS[j]
            nc.vector.quantize_mx(oc[:, c0 : c0 + n].bitcast(FP8X4), op[:, c0 : c0 + n], ob[j][:])
            nc.sync.dma_start(out_words[:, c0 : c0 + n], oc[:, c0 : c0 + n].bitcast(I32))

        for j, (c0, n) in enumerate(OUT_CHUNKS):
            for t in range(PACK):
                nc.vector.tensor_tensor(half[t][:, c0 : c0 + n], hwin[t][:].indirect(entries(n3_t, c0, n)), own(t, c0, n), ALU.add)
            if j > 0:
                finish(j - 1)
            for t in range(PACK):
                nc.vector.tensor_tensor(res[j][:, t, :], hwin[t][:].indirect(entries(n4_t, c0, n)), half[t][:, c0 : c0 + n], ALU.add)
            nc.sync.dma_start(out_rows[:, :, c0 : c0 + n], res[j][:])
            if j < len(OUT_CHUNKS) - 1:
                nc.scalar.copy(woven(ob[j]), unwoven(res[j][:]))
            else:
                nc.vector.tensor_copy(woven(ob[j]), unwoven(res[j][:]))
        finish(len(OUT_CHUNKS) - 1)
        for q in range(4):
            queue = nc.scalar if q % 2 == 0 else nc.sync
            queue.dma_start(out_2[0, 4 * q : 4 * q + 4, :].bitcast(I32), op[32 * q : 32 * q + 4, :].bitcast(I32))
